import numpy as np, ml_dtypes
CORES = [10,14,66,70,74,78,82,86,90,94,106,110]
N = 12
S, B = 2, 512
def setup_inputs(rng):
    return {"x": rng.standard_normal((N, 128, S * B), dtype=np.float32).astype(ml_dtypes.bfloat16), "gate": (0.9375 + 0.03125 * rng.standard_normal((N, 128, S * B), dtype=np.float32)).astype(ml_dtypes.bfloat16)}
def setup_inputs_big(rng):
    d = setup_inputs(rng)
    for k in ("x",): d[k] = (d[k].astype(np.float32) * 1048576.0).astype(d[k].dtype)
    return d
def setup_inputs_small(rng):
    d = setup_inputs(rng)
    for k in ("x",): d[k] = (d[k].astype(np.float32) * (1 / 1048576.0)).astype(d[k].dtype)
    return d
def setup_inputs_apart(rng):
    d = setup_inputs(rng)
    f = (10.0 ** rng.permutation(np.linspace(-1.5, 1.5, N))).astype(np.float32).reshape(N, 1, 1)
    for k in ("x",): d[k] = (d[k].astype(np.float32) * f).astype(d[k].dtype)
    return d
def reference(x, gate):
    X, GATE = x.astype(np.float64), gate.astype(np.float64)
    y = np.zeros((N, 128, S * B)); h = np.zeros((128, B))
    for r in range(N):
        for s in range(S):
            h = GATE[r][:, B * s:B * s + B] * h + X[r][:, B * s:B * s + B]
            y[r][:, B * s:B * s + B] = h
    return {"y": y.astype(ml_dtypes.bfloat16)}

@@ -1,0 +1,289 @@
+from concourse.bass import DstId, RemoteDMATransfer
+from concourse.mybir import AluOpType
+
+B = 512
+K = 4
+W = B // K
+NEAR = 4
+
+SCRATCH = {
+    "G": ("sbuf", [128, 2 * B], "bfloat16"),
+    "X": ("sbuf", [128, 2 * B], "bfloat16"),
+    "AB": ("sbuf", [128, 2 * B], "bfloat16"),
+    "land1": ("sbuf", [128, 6 * 2 * W], "bfloat16"),
+    "Hbuf": ("sbuf", [128, 7 * W], "bfloat16"),
+    "cland": ("sbuf", [128, W], "bfloat16"),
+    "hland": ("sbuf", [128, B], "bfloat16"),
+    "ybuf": ("sbuf", [128, 2 * B], "bfloat16"),
+    "tmpS": ("sbuf", [128, 6 * W], "float32"),
+    "pg1": ("psum", [128, B], "float32"),
+    "pg0": ("psum", [128, B], "float32"),
+    "pt": ("psum", [128, B], "float32"),
+    "pm": ("psum", [128, B], "float32"),
+    "pc": ("psum", [128, 12 * W], "float32"),
+}
+SEMAPHORES = ["ldg", "ldx0", "ldx1", "v", "car", "s2", "ls", "st0", "st1"] + ["s1_%d" % m for m in range(6)]
+
+
+def _bits(mask):
+    return [1 << i for i in range(mask.bit_length()) if (mask >> i) & 1]
+
+
+def _share(bits, n):
+    size = 1
+    while size * 2 * n <= len(bits):
+        size *= 2
+    return [sum(bits[i * size:(i + 1) * size]) for i in range(n)], size
+
+
+def _plan(T, topo):
+    cores = list(T.cores)
+    n = len(cores)
+    groups = [list(range(n // 2)), list(range(n // 2, n))]
+    chip = [topo.chip(c) for c in cores]
+    lo = groups[0][:K]
+    hi = []
+    for o in lo:
+        free = [r for r in groups[1][:-1] if r not in hi]
+        hi.append(min(free, key=lambda r: (
+            0 if (topo.mates(chip[o], chip[r]) or topo.same_plane(chip[o], chip[r])) else 1,
+            0 if topo.die(cores[o]) == topo.die(cores[r]) else 1)))
+    owners = [lo, hi]
+
+    def engines(q):
+        far, near = None, 0
+        for r in range(n):
+            if r == q:
+                continue
+            m = topo.mask(cores[q], cores[r])
+            if chip[r] != chip[q]:
+                far = m if far is None else far & m
+            else:
+                near |= m
+        return _bits(far), [b for b in _bits(near) if not (b & far)][:NEAR]
+
+    def pairs(q, off, on, per_call, on_last):
+        farb, nearb = engines(q)
+        calls = []
+        for i in range(0, len(off), per_call):
+            part = off[i:i + per_call]
+            masks, size = _share(farb, len(part))
+            calls.append([(key, r, masks[k], size) for k, (key, r) in enumerate(part)])
+        if on:
+            masks, size = _share(nearb, len(on))
+            extra = [(key, r, masks[k], size) for k, (key, r) in enumerate(on)]
+            if calls:
+                calls[-1 if on_last else 0].extend(extra)
+            else:
+                calls.append(extra)
+        return calls
+
+    def s1(q):
+        if q == n - 1:
+            return []
+        own = owners[0 if q in groups[0] else 1]
+        dst = [(j, own[j]) for j in range(K) if own[j] != q]
+        return pairs(q, [d for d in dst if chip[d[1]] != chip[q]], [d for d in dst if chip[d[1]] == chip[q]], 2, False)
+
+    def s2(o):
+        gi = 0 if o in groups[0] else 1
+        grp = groups[gi]
+        dst = [(i, r) for i, r in enumerate(grp) if r != o and r != 0]
+        off = [d for d in dst if chip[d[1]] != chip[o]]
+        on = [d for d in dst if chip[d[1]] == chip[o]]
+        chs = []
+        for r in grp:
+            if chip[r] not in chs:
+                chs.append(chip[r])
+        p = chs.index(chip[o])
+        off.sort(key=lambda d: (p - chs.index(chip[d[1]])) % len(chs))
+        return pairs(o, off, on, len(off) if gi == 0 else 2, True)
+
+    return cores, groups, owners, engines, s1, s2
+
+
+def rank_program(g, core, T, topo):
+    rank = T.rank_of(core)
+    if rank is None:
+        return
+    cores, groups, owners, engines, s1, s2 = _plan(T, topo)
+    n = len(cores)
+    gi = 0 if rank in groups[0] else 1
+    grp = groups[gi]
+    me = grp.index(rank)
+    S, V = T.sem, g.vector
+    mult, add = AluOpType.mult, AluOpType.add
+    vc, vseen, gseen, ls = [0], [0], [0], [0]
+
+    def vdo(ins):
+        ins.then_inc(S.v, 1)
+        vc[0] += 1
+        return vc[0]
+
+    def need(i):
+        if i > vseen[0]:
+            V.wait_ge(S.v, i)
+            vseen[0] = i
+
+    def gneed(i):
+        if i > gseen[0]:
+            g.wait_ge(S.v, i)
+            gseen[0] = i
+
+    def tt(out, a, b, op):
+        return vdo(V.tensor_tensor(out, a, b, op))
+
+    def sl(j, base=0):
+        return slice(base + j * W, base + (j + 1) * W)
+
+    def fused(items):
+        trs = []
+        for r, mask, size, src, dst, sem in items:
+            rid, pid, _se = topo.addr(cores[r])
+            trs.append(RemoteDMATransfer(dst_ids=[DstId(rid=rid, pnc=pid)], dma_engine_mask=mask, remote_sem=sem,
+                                         src=src, dst=dst))
+            ls[0] += size
+        g.remote_dma_fused(trs, local_sem=S.ls)
+
+    g.sync.dma_start(T.G[:], T.gate[:]).then_inc(S.ldg, 16)
+    g.scalar.dma_start(T.X[:, 0:B], T.x[:, 0:B]).then_inc(S.ldx0, 16)
+    g.scalar.dma_start(T.X[:, B:2 * B], T.x[:, B:2 * B]).then_inc(S.ldx1, 16)
+
+    calls1 = s1(rank)
+    V.wait_ge(S.ldg, 16)
+    i_g1 = vdo(V.tensor_copy(T.pg1[:], T.G[:, B:2 * B]))
+    bidx = {}
+    if rank != n - 1:
+        chunks = [[t[0] for t in c] for c in calls1]
+        rest = [j for j in range(K) if all(j not in c for c in chunks)]
+        if rest:
+            chunks.append(rest)
+        need(i_g1)
+        if rank != 0:
+            for c in chunks:
+                for j in c:
+                    tt(T.AB[:, sl(2 * j)], T.pg1[:, sl(j)], T.G[:, sl(j)], mult)
+        V.wait_ge(S.ldx0, 16)
+        for k, c in enumerate(chunks):
+            ti = [tt(T.pt[:, sl(j)], T.pg1[:, sl(j)], T.X[:, sl(j)], mult) for j in c]
+            if k == 0:
+                V.wait_ge(S.ldx1, 16)
+            for j, i in zip(c, ti):
+                need(i)
+                bidx[j] = tt(T.AB[:, sl(2 * j + 1)], T.pt[:, sl(j)], T.X[:, sl(j, B)], add)
+        for c in calls1:
+            gneed(max(bidx[t[0]] for t in c))
+            lo_col = W if rank == 0 else 0
+            fused([(r, mask, size, T.AB[:, 2 * W * j + lo_col:2 * W * (j + 1)],
+                    T.land1[:, 2 * W * me + lo_col:2 * W * (me + 1)], S["s1_%d" % me]) for j, r, mask, size in c])
+    else:
+        V.wait_ge(S.ldx0, 16)
+        V.wait_ge(S.ldx1, 16)
+
+    i_own = 0
+    if rank == 0:
+        need(max(bidx.values()))
+        i_y = tt(T.ybuf[:, B:2 * B], T.pt[:], T.X[:, B:2 * B], add)
+        g.sync.wait_ge(S.ldx0, 16)
+        g.sync.dma_start(T.y[:, 0:B], T.X[:, 0:B]).then_inc(S.st0, 16)
+        g.scalar.wait_ge(S.v, i_y)
+        g.scalar.dma_start(T.y[:, B:2 * B], T.ybuf[:, B:2 * B]).then_inc(S.st1, 16)
+    else:
+        i_g0 = vdo(V.tensor_copy(T.pg0[:], T.G[:, 0:B]))
+
+    if rank in owners[gi]:
+        j = owners[gi].index(rank)
+        arrived = {}
+        for m, q in enumerate(grp):
+            for c in s1(q):
+                for t in c:
+                    if t[1] == rank:
+                        arrived[m] = t[3]
+
+        def comp(m):
+            if grp[m] == rank:
+                need(bidx[j])
+                return T.AB[:, sl(2 * j)], T.AB[:, sl(2 * j + 1)]
+            V.wait_ge(S["s1_%d" % m], arrived[m])
+            return T.land1[:, sl(2 * m)], T.land1[:, sl(2 * m + 1)]
+
+        def hout(i):
+            return T.hland[:, sl(j)] if i == me else T.Hbuf[:, sl(i)]
+
+        calls2 = s2(rank)
+        hloc, hidx = {}, {}
+        if gi == 0:
+            hloc[1] = comp(0)[1]
+            hidx[1] = 0
+            for m in range(1, len(grp)):
+                a, b = comp(m)
+                p = T.pc[:, sl(10 + m % 2)]
+                need(hidx[m])
+                need(tt(p, a, hloc[m], mult))
+                hloc[m + 1] = hout(m + 1)
+                hidx[m + 1] = tt(hloc[m + 1], p, b, add)
+            last = len(grp)
+            if me == 1:
+                i_own = vdo(V.tensor_copy(T.hland[:, sl(j)], hloc[1]))
+            elif me > 1:
+                i_own = hidx[me]
+            gneed(hidx[last])
+            farb, _nearb = engines(rank)
+            rid, pid, _se = topo.addr(cores[owners[1][j]])
+            g.remote_dma(T.cland[:], hloc[last], S.car, S.ls, pid, rid, sum(farb))
+            ls[0] += len(farb)
+            if me != 0:
+                g.wait_ge(S.s1_0, arrived[0])
+            for c in calls2:
+                fused([(r, mask, size, hloc[i], T.hland[:, sl(j)], S.s2) for i, r, mask, size in c])
+        else:
+            a, b = comp(0)
+            ia = vdo(V.tensor_copy(T.pc[:, sl(0)], a))
+            ib = vdo(V.tensor_copy(T.pc[:, sl(5)], b))
+            for m in range(1, len(grp) - 1):
+                a, b = comp(m)
+                p = T.pc[:, sl(10 + m % 2)]
+                need(ib)
+                ip = tt(p, a, T.pc[:, sl(5 + m - 1)], mult)
+                need(ia)
+                ia = tt(T.pc[:, sl(m)], a, T.pc[:, sl(m - 1)], mult)
+                need(ip)
+                ib = tt(T.pc[:, sl(5 + m)], p, b, add)
+            need(max(ia, ib))
+            ncar = len(engines(owners[0][j])[0])
+            V.wait_ge(S.car, ncar)
+            g.wait_ge(S.car, ncar)
+            for c in calls2 + [[(me, rank, 0, 0)]]:
+                todo = [t[0] for t in c if t[0] != 0]
+                ti = [tt(T.tmpS[:, sl(i)], T.pc[:, sl(i - 1)], T.cland[:], mult) for i in todo]
+                done = 0
+                for i, k in zip(todo, ti):
+                    need(k)
+                    hloc[i] = hout(i)
+                    done = tt(hloc[i], T.tmpS[:, sl(i)], T.pc[:, sl(5 + i - 1)], add)
+                hloc[0] = T.cland[:]
+                if c[0][1] == rank:
+                    i_own = done if me != 0 else vdo(V.tensor_copy(T.hland[:, sl(j)], T.cland[:]))
+                else:
+                    gneed(done)
+                    fused([(r, mask, size, hloc[i], T.hland[:, sl(j)], S.s2) for i, r, mask, size in c])
+
+    if rank != 0:
+        total = sum(t[3] for o in owners[gi] if o != rank for c in s2(o) for t in c if t[1] == rank)
+        V.wait_ge(S.s2, total)
+        need(max(i_own, i_g0))
+        need(tt(T.pm[:], T.pg0[:], T.hland[:], mult))
+        i_y0 = tt(T.ybuf[:, 0:B], T.pm[:], T.X[:, 0:B], add)
+        need(i_y0)
+        need(tt(T.pt[:], T.pg1[:], T.ybuf[:, 0:B], mult))
+        i_y1 = tt(T.ybuf[:, B:2 * B], T.pt[:], T.X[:, B:2 * B], add)
+        g.sync.wait_ge(S.v, i_y0)
+        g.sync.dma_start(T.y[:, 0:B], T.ybuf[:, 0:B]).then_inc(S.st0, 16)
+        g.scalar.wait_ge(S.v, i_y1)
+        g.scalar.dma_start(T.y[:, B:2 * B], T.ybuf[:, B:2 * B]).then_inc(S.st1, 16)
+
+    g.sync.wait_ge(S.st0, 16)
+    g.scalar.wait_ge(S.st1, 16)
+    g.wait_ge(S.v, vc[0])
+    if ls[0]:
+        g.wait_ge(S.ls, ls[0])

@@ -12,17 +12,21 @@ SCRATCH = {
     "AB": ("sbuf", [128, 2 * B], "bfloat16"),
     "land1": ("sbuf", [128, 6 * 2 * W], "bfloat16"),
     "Hbuf": ("sbuf", [128, 7 * W], "bfloat16"),
-    "cland": ("sbuf", [128, W], "bfloat16"),
+    "MB": ("sbuf", [128, 6 * 2 * W], "bfloat16"),
+    "mland": ("sbuf", [128, K * 2 * W], "bfloat16"),
+    "cland": ("sbuf", [128, B], "bfloat16"),
     "hland": ("sbuf", [128, B], "bfloat16"),
     "ybuf": ("sbuf", [128, 2 * B], "bfloat16"),
-    "tmpS": ("sbuf", [128, 6 * W], "float32"),
+    "Q0": ("sbuf", [128, B], "float32"),
+    "pa": ("psum", [128, B], "float32"),
     "pg1": ("psum", [128, B], "float32"),
     "pg0": ("psum", [128, B], "float32"),
     "pt": ("psum", [128, B], "float32"),
     "pm": ("psum", [128, B], "float32"),
-    "pc": ("psum", [128, 12 * W], "float32"),
+    "pc": ("psum", [128, B], "float32"),
 }
-SEMAPHORES = ["ldg", "ldx0", "ldx1", "v", "car", "s2", "ls", "st0", "st1"] + ["s1_%d" % m for m in range(6)]
+SEMAPHORES = (["ldg", "ldx0", "ldx1", "v", "car", "ls", "st0", "st1"] + ["s1_%d" % m for m in range(6)]
+              + ["s2_%d" % j for j in range(K)])
 
 
 def _bits(mask):
@@ -41,14 +45,7 @@ def _plan(T, topo):
     n = len(cores)
     groups = [list(range(n // 2)), list(range(n // 2, n))]
     chip = [topo.chip(c) for c in cores]
-    lo = groups[0][:K]
-    hi = []
-    for o in lo:
-        free = [r for r in groups[1][:-1] if r not in hi]
-        hi.append(min(free, key=lambda r: (
-            0 if (topo.mates(chip[o], chip[r]) or topo.same_plane(chip[o], chip[r])) else 1,
-            0 if topo.die(cores[o]) == topo.die(cores[r]) else 1)))
-    owners = [lo, hi]
+    owners = [groups[0][:K], groups[1][:K]]
 
     def engines(q):
         far, near = None, 0
@@ -62,7 +59,9 @@ def _plan(T, topo):
                 near |= m
         return _bits(far), [b for b in _bits(near) if not (b & far)][:NEAR]
 
-    def pairs(q, off, on, per_call, on_last):
+    def pairs(q, dst, per_call):
+        off = [d for d in dst if chip[d[1]] != chip[q]]
+        on = [d for d in dst if chip[d[1]] == chip[q]]
         farb, nearb = engines(q)
         calls = []
         for i in range(0, len(off), per_call):
@@ -73,7 +72,7 @@ def _plan(T, topo):
             masks, size = _share(nearb, len(on))
             extra = [(key, r, masks[k], size) for k, (key, r) in enumerate(on)]
             if calls:
-                calls[-1 if on_last else 0].extend(extra)
+                calls[0].extend(extra)
             else:
                 calls.append(extra)
         return calls
@@ -82,22 +81,16 @@ def _plan(T, topo):
         if q == n - 1:
             return []
         own = owners[0 if q in groups[0] else 1]
-        dst = [(j, own[j]) for j in range(K) if own[j] != q]
-        return pairs(q, [d for d in dst if chip[d[1]] != chip[q]], [d for d in dst if chip[d[1]] == chip[q]], 2, False)
+        return pairs(q, [(j, own[j]) for j in range(K) if own[j] != q], 2)
 
     def s2(o):
         gi = 0 if o in groups[0] else 1
-        grp = groups[gi]
-        dst = [(i, r) for i, r in enumerate(grp) if r != o and r != 0]
-        off = [d for d in dst if chip[d[1]] != chip[o]]
-        on = [d for d in dst if chip[d[1]] == chip[o]]
-        chs = []
-        for r in grp:
-            if chip[r] not in chs:
-                chs.append(chip[r])
-        p = chs.index(chip[o])
-        off.sort(key=lambda d: (p - chs.index(chip[d[1]])) % len(chs))
-        return pairs(o, off, on, len(off) if gi == 0 else 2, True)
+        dst = [(i, r) for i, r in enumerate(groups[gi]) if r != o and i != 0]
+        if gi == 1:
+            return pairs(o, dst, 2)
+        early = [d for d in dst if d[1] in owners[0]]
+        late = [d for d in dst if d[1] not in owners[0]]
+        return pairs(o, early, max(1, len(early))) + pairs(o, late, 1)
 
     return cores, groups, owners, engines, s1, s2
 
@@ -136,12 +129,14 @@ def rank_program(g, core, T, topo):
     def sl(j, base=0):
         return slice(base + j * W, base + (j + 1) * W)
 
+    def did(r):
+        rid, pid, _se = topo.addr(cores[r])
+        return DstId(rid=rid, pnc=pid)
+
     def fused(items):
         trs = []
         for r, mask, size, src, dst, sem in items:
-            rid, pid, _se = topo.addr(cores[r])
-            trs.append(RemoteDMATransfer(dst_ids=[DstId(rid=rid, pnc=pid)], dma_engine_mask=mask, remote_sem=sem,
-                                         src=src, dst=dst))
+            trs.append(RemoteDMATransfer(dst_ids=[did(r)], dma_engine_mask=mask, remote_sem=sem, src=src, dst=dst))
             ls[0] += size
         g.remote_dma_fused(trs, local_sem=S.ls)
 
@@ -151,14 +146,13 @@ def rank_program(g, core, T, topo):
 
     calls1 = s1(rank)
     V.wait_ge(S.ldg, 16)
-    i_g1 = vdo(V.tensor_copy(T.pg1[:], T.G[:, B:2 * B]))
+    need(vdo(V.tensor_copy(T.pg1[:], T.G[:, B:2 * B])))
     bidx = {}
     if rank != n - 1:
         chunks = [[t[0] for t in c] for c in calls1]
         rest = [j for j in range(K) if all(j not in c for c in chunks)]
         if rest:
             chunks.append(rest)
-        need(i_g1)
         if rank != 0:
             for c in chunks:
                 for j in c:
@@ -191,6 +185,7 @@ def rank_program(g, core, T, topo):
     else:
         i_g0 = vdo(V.tensor_copy(T.pg0[:], T.G[:, 0:B]))
 
+    mA, mB, midx = {}, {}, {}
     if rank in owners[gi]:
         j = owners[gi].index(rank)
         arrived = {}
@@ -207,73 +202,91 @@ def rank_program(g, core, T, topo):
             V.wait_ge(S["s1_%d" % m], arrived[m])
             return T.land1[:, sl(2 * m)], T.land1[:, sl(2 * m + 1)]
 
-        def hout(i):
-            return T.hland[:, sl(j)] if i == me else T.Hbuf[:, sl(i)]
-
         calls2 = s2(rank)
-        hloc, hidx = {}, {}
         if gi == 0:
+            hloc, hidx = {}, {}
+            last = len(grp)
             hloc[1] = comp(0)[1]
             hidx[1] = 0
-            for m in range(1, len(grp)):
+            for m in range(1, last):
                 a, b = comp(m)
-                p = T.pc[:, sl(10 + m % 2)]
+                p = T.pc[:, sl(m % 2)]
                 need(hidx[m])
                 need(tt(p, a, hloc[m], mult))
-                hloc[m + 1] = hout(m + 1)
+                hloc[m + 1] = T.hland[:, sl(j)] if m + 1 == me else T.Hbuf[:, sl(m + 1)]
                 hidx[m + 1] = tt(hloc[m + 1], p, b, add)
-            last = len(grp)
             if me == 1:
                 i_own = vdo(V.tensor_copy(T.hland[:, sl(j)], hloc[1]))
             elif me > 1:
                 i_own = hidx[me]
-            gneed(hidx[last])
-            farb, _nearb = engines(rank)
-            rid, pid, _se = topo.addr(cores[owners[1][j]])
-            g.remote_dma(T.cland[:], hloc[last], S.car, S.ls, pid, rid, sum(farb))
-            ls[0] += len(farb)
             if me != 0:
                 g.wait_ge(S.s1_0, arrived[0])
             for c in calls2:
-                fused([(r, mask, size, hloc[i], T.hland[:, sl(j)], S.s2) for i, r, mask, size in c])
+                gneed(max(hidx[t[0]] for t in c))
+                fused([(r, mask, size, hloc[i], T.hland[:, sl(j)], S["s2_%d" % j]) for i, r, mask, size in c])
+            gneed(hidx[last])
+            farb, _nearb = engines(rank)
+            g.remote_dma_fused([RemoteDMATransfer(
+                dst_ids=[did(r) for r in groups[1]], dma_engine_mask=sum(farb), remote_sem=S.car,
+                srcs=[hloc[last]], dsts=[T.cland[:, sl(j)] for r in groups[1]], alu_op=0)], local_sem=S.ls)
+            ls[0] += len(farb)
         else:
-            a, b = comp(0)
-            ia = vdo(V.tensor_copy(T.pc[:, sl(0)], a))
-            ib = vdo(V.tensor_copy(T.pc[:, sl(5)], b))
+            mA[1], mB[1] = comp(0)
+            mfull = {1: T.AB[:, 2 * W * j:2 * W * (j + 1)] if me == 0 else T.land1[:, 0:2 * W]}
+            midx[1] = bidx[j] if me == 0 else 0
             for m in range(1, len(grp) - 1):
                 a, b = comp(m)
-                p = T.pc[:, sl(10 + m % 2)]
-                need(ib)
-                ip = tt(p, a, T.pc[:, sl(5 + m - 1)], mult)
-                need(ia)
-                ia = tt(T.pc[:, sl(m)], a, T.pc[:, sl(m - 1)], mult)
+                p = T.pc[:, sl(m % 2)]
+                need(midx[m])
+                ip = tt(p, a, mB[m], mult)
+                mA[m + 1], mB[m + 1] = T.MB[:, sl(2 * m + 2)], T.MB[:, sl(2 * m + 3)]
+                mfull[m + 1] = T.MB[:, 2 * W * (m + 1):2 * W * (m + 2)]
+                tt(mA[m + 1], a, mA[m], mult)
                 need(ip)
-                ib = tt(T.pc[:, sl(5 + m)], p, b, add)
-            need(max(ia, ib))
-            ncar = len(engines(owners[0][j])[0])
-            V.wait_ge(S.car, ncar)
-            g.wait_ge(S.car, ncar)
-            for c in calls2 + [[(me, rank, 0, 0)]]:
-                todo = [t[0] for t in c if t[0] != 0]
-                ti = [tt(T.tmpS[:, sl(i)], T.pc[:, sl(i - 1)], T.cland[:], mult) for i in todo]
-                done = 0
-                for i, k in zip(todo, ti):
-                    need(k)
-                    hloc[i] = hout(i)
-                    done = tt(hloc[i], T.tmpS[:, sl(i)], T.pc[:, sl(5 + i - 1)], add)
-                hloc[0] = T.cland[:]
-                if c[0][1] == rank:
-                    i_own = done if me != 0 else vdo(V.tensor_copy(T.hland[:, sl(j)], T.cland[:]))
-                else:
-                    gneed(done)
-                    fused([(r, mask, size, hloc[i], T.hland[:, sl(j)], S.s2) for i, r, mask, size in c])
+                midx[m + 1] = tt(mB[m + 1], p, b, add)
+            if me != 0:
+                g.wait_ge(S.s1_0, arrived[0])
+            for c in calls2:
+                gneed(max(midx[t[0]] for t in c))
+                fused([(r, mask, size, mfull[i], T.mland[:, 2 * W * j:2 * W * (j + 1)], S["s2_%d" % j])
+                       for i, r, mask, size in c])
 
     if rank != 0:
-        total = sum(t[3] for o in owners[gi] if o != rank for c in s2(o) for t in c if t[1] == rank)
-        V.wait_ge(S.s2, total)
-        need(max(i_own, i_g0))
-        need(tt(T.pm[:], T.pg0[:], T.hland[:], mult))
-        i_y0 = tt(T.ybuf[:, 0:B], T.pm[:], T.X[:, 0:B], add)
+        cnt = {}
+        for jj, o in enumerate(owners[gi]):
+            for c in (s2(o) if o != rank else []):
+                for t in c:
+                    if t[1] == rank:
+                        cnt[jj] = t[3]
+        ncar = sum(len(engines(o)[0]) for o in owners[0])
+        need(i_g0)
+        if gi == 1 and me != 0:
+            for jj in range(K):
+                if jj in cnt:
+                    V.wait_ge(S["s2_%d" % jj], cnt[jj])
+                    asrc, bsrc = T.mland[:, sl(2 * jj)], T.mland[:, sl(2 * jj + 1)]
+                else:
+                    need(midx[me])
+                    asrc, bsrc = mA[me], mB[me]
+                iq = tt(T.pm[:, sl(jj)], T.pg0[:, sl(jj)], bsrc, mult)
+                tt(T.pa[:, sl(jj)], T.pg0[:, sl(jj)], asrc, mult)
+                need(iq)
+                ic = tt(T.Q0[:, sl(jj)], T.pm[:, sl(jj)], T.X[:, sl(jj)], add)
+            V.wait_ge(S.car, ncar)
+            need(ic)
+            need(tt(T.pt[:], T.pa[:], T.cland[:], mult))
+            i_y0 = tt(T.ybuf[:, 0:B], T.pt[:], T.Q0[:], add)
+        else:
+            if gi == 1:
+                V.wait_ge(S.car, ncar)
+                h = T.cland
+            else:
+                for jj in cnt:
+                    V.wait_ge(S["s2_%d" % jj], cnt[jj])
+                need(i_own)
+                h = T.hland
+            need(tt(T.pm[:], T.pg0[:], h[:], mult))
+            i_y0 = tt(T.ybuf[:, 0:B], T.pm[:], T.X[:, 0:B], add)
         need(i_y0)
         need(tt(T.pt[:], T.pg1[:], T.ybuf[:, 0:B], mult))
         i_y1 = tt(T.ybuf[:, B:2 * B], T.pt[:], T.X[:, B:2 * B], add)

@@ -81,7 +81,21 @@ def _plan(T, topo):
         if q == n - 1:
             return []
         own = owners[0 if q in groups[0] else 1]
-        return pairs(q, [(j, own[j]) for j in range(K) if own[j] != q], 2)
+        dst = [(j, own[j]) for j in range(K) if own[j] != q]
+        off = [d for d in dst if chip[d[1]] != chip[q]]
+        on = [d for d in dst if chip[d[1]] == chip[q]]
+        farb, nearb = engines(q)
+        ncalls = (len(off) + 1) // 2
+        per = len(farb) // max(1, ncalls)
+        calls = []
+        for i in range(ncalls):
+            part = off[2 * i:2 * i + 2]
+            masks, size = _share(farb[i * per:(i + 1) * per], len(part))
+            calls.append([(key, r, masks[k], size) for k, (key, r) in enumerate(part)])
+        if on:
+            masks, size = _share(nearb, len(on))
+            calls.append([(key, r, masks[k], size) for k, (key, r) in enumerate(on)])
+        return calls
 
     def s2(o):
         gi = 0 if o in groups[0] else 1
@@ -146,20 +160,19 @@ def rank_program(g, core, T, topo):
 
     calls1 = s1(rank)
     V.wait_ge(S.ldg, 16)
-    need(vdo(V.tensor_copy(T.pg1[:], T.G[:, B:2 * B])))
     bidx = {}
     if rank != n - 1:
         chunks = [[t[0] for t in c] for c in calls1]
         rest = [j for j in range(K) if all(j not in c for c in chunks)]
         if rest:
             chunks.append(rest)
-        if rank != 0:
-            for c in chunks:
-                for j in c:
-                    tt(T.AB[:, sl(2 * j)], T.pg1[:, sl(j)], T.G[:, sl(j)], mult)
-        V.wait_ge(S.ldx0, 16)
         for k, c in enumerate(chunks):
-            ti = [tt(T.pt[:, sl(j)], T.pg1[:, sl(j)], T.X[:, sl(j)], mult) for j in c]
+            if rank != 0:
+                for j in c:
+                    tt(T.AB[:, sl(2 * j)], T.G[:, sl(j, B)], T.G[:, sl(j)], mult)
+            if k == 0:
+                V.wait_ge(S.ldx0, 16)
+            ti = [tt(T.pt[:, sl(j)], T.G[:, sl(j, B)], T.X[:, sl(j)], mult) for j in c]
             if k == 0:
                 V.wait_ge(S.ldx1, 16)
             for j, i in zip(c, ti):
@@ -183,6 +196,7 @@ def rank_program(g, core, T, topo):
         g.scalar.wait_ge(S.v, i_y)
         g.scalar.dma_start(T.y[:, B:2 * B], T.ybuf[:, B:2 * B]).then_inc(S.st1, 16)
     else:
+        vdo(V.tensor_copy(T.pg1[:], T.G[:, B:2 * B]))
         i_g0 = vdo(V.tensor_copy(T.pg0[:], T.G[:, 0:B]))
 
     mA, mB, midx = {}, {}, {}

@@ -1,5 +1,5 @@
 from concourse.bass import DstId, RemoteDMATransfer
-from concourse.mybir import AluOpType
+from concourse.mybir import AluOpType, ActivationFunctionType
 
 B = 512
 K = 4
@@ -14,10 +14,13 @@ SCRATCH = {
     "Hbuf": ("sbuf", [128, 7 * W], "bfloat16"),
     "MB": ("sbuf", [128, 6 * 2 * W], "bfloat16"),
     "mland": ("sbuf", [128, K * 2 * W], "bfloat16"),
+    "nland": ("sbuf", [128, K * 2 * W], "bfloat16"),
     "cland": ("sbuf", [128, B], "bfloat16"),
     "hland": ("sbuf", [128, B], "bfloat16"),
     "ybuf": ("sbuf", [128, 2 * B], "bfloat16"),
+    "Qn": ("sbuf", [128, B], "float32"),
     "Q0": ("sbuf", [128, B], "float32"),
+    "pn": ("psum", [128, B], "float32"),
     "pa": ("psum", [128, B], "float32"),
     "pg1": ("psum", [128, B], "float32"),
     "pg0": ("psum", [128, B], "float32"),
@@ -25,8 +28,8 @@ SCRATCH = {
     "pm": ("psum", [128, B], "float32"),
     "pc": ("psum", [128, B], "float32"),
 }
-SEMAPHORES = (["ldg", "ldx0", "ldx1", "v", "car", "ls", "st0", "st1"] + ["s1_%d" % m for m in range(6)]
-              + ["s2_%d" % j for j in range(K)])
+SEMAPHORES = (["ldg", "ldx0", "ldx1", "v", "a0", "a1", "nb", "c0", "c1", "ls", "st0", "st1"]
+              + ["s1_%d" % m for m in range(6)] + ["s2_%d" % j for j in range(K)])
 
 
 def _bits(mask):
@@ -40,12 +43,19 @@ def _share(bits, n):
     return [sum(bits[i * size:(i + 1) * size]) for i in range(n)], size
 
 
+def _half(j):
+    return j * 2 // K
+
+
 def _plan(T, topo):
     cores = list(T.cores)
     n = len(cores)
     groups = [list(range(n // 2)), list(range(n // 2, n))]
     chip = [topo.chip(c) for c in cores]
     owners = [groups[0][:K], groups[1][:K]]
+    rest0 = [r for r in groups[0] if r not in owners[0]]
+    rest1 = [r for r in groups[1] if r not in owners[1]]
+    feed = {rest0[1]: rest0[0], groups[1][1]: groups[1][0], rest1[1]: rest1[0]}
 
     def engines(q):
         far, near = None, 0
@@ -57,12 +67,30 @@ def _plan(T, topo):
                 far = m if far is None else far & m
             else:
                 near |= m
-        return _bits(far), [b for b in _bits(near) if not (b & far)][:NEAR]
+        stay = [b for b in _bits(near) if not (b & far)]
+        return _bits(far), stay[:NEAR], stay
+
+    duo2, solo2 = [], []
+    for r in groups[1]:
+        same = [q for q in groups[1] if chip[q] == chip[r]]
+        if same[0] != r:
+            continue
+        if len(same) == 2 and (n - 1) not in same:
+            duo2.append(same)
+        else:
+            solo2.extend(same)
+    swap = {}
+    for duo in [rest0] + duo2:
+        swap[duo[0]] = (0, duo[1])
+        swap[duo[1]] = (1, duo[0])
+
+    def cdst(j):
+        return [duo[_half(j)] for duo in duo2] + solo2
 
     def pairs(q, dst, per_call):
         off = [d for d in dst if chip[d[1]] != chip[q]]
         on = [d for d in dst if chip[d[1]] == chip[q]]
-        farb, nearb = engines(q)
+        farb, nearb, _all = engines(q)
         calls = []
         for i in range(0, len(off), per_call):
             part = off[i:i + per_call]
@@ -78,13 +106,13 @@ def _plan(T, topo):
         return calls
 
     def s1(q):
-        if q == n - 1:
+        if q in rest1:
             return []
         own = owners[0 if q in groups[0] else 1]
         dst = [(j, own[j]) for j in range(K) if own[j] != q]
         off = [d for d in dst if chip[d[1]] != chip[q]]
         on = [d for d in dst if chip[d[1]] == chip[q]]
-        farb, nearb = engines(q)
+        farb, nearb, _all = engines(q)
         ncalls = (len(off) + 1) // 2
         per = len(farb) // max(1, ncalls)
         calls = []
@@ -99,28 +127,27 @@ def _plan(T, topo):
 
     def s2(o):
         gi = 0 if o in groups[0] else 1
-        dst = [(i, r) for i, r in enumerate(groups[gi]) if r != o and i != 0]
         if gi == 1:
+            dst = [(min(i, K), r) for i, r in enumerate(groups[1]) if r != o and i >= 2]
             return pairs(o, dst, 2)
-        early = [d for d in dst if d[1] in owners[0]]
-        late = [d for d in dst if d[1] not in owners[0]]
-        return pairs(o, early, max(1, len(early))) + pairs(o, late, 1)
+        early = [(i, r) for i, r in enumerate(groups[0]) if r != o and i != 0 and r in owners[0]]
+        return pairs(o, early, max(1, len(early)))
 
-    return cores, groups, owners, engines, s1, s2
+    return cores, groups, owners, rest0, feed, swap, cdst, engines, s1, s2
 
 
 def rank_program(g, core, T, topo):
     rank = T.rank_of(core)
     if rank is None:
         return
-    cores, groups, owners, engines, s1, s2 = _plan(T, topo)
+    cores, groups, owners, rest0, feed, swap, cdst, engines, s1, s2 = _plan(T, topo)
     n = len(cores)
     gi = 0 if rank in groups[0] else 1
     grp = groups[gi]
     me = grp.index(rank)
     S, V = T.sem, g.vector
     mult, add = AluOpType.mult, AluOpType.add
-    vc, vseen, gseen, ls = [0], [0], [0], [0]
+    vc, vseen, gseen, ls, nst = [0], [0], [0], [0], [0]
 
     def vdo(ins):
         ins.then_inc(S.v, 1)
@@ -157,6 +184,10 @@ def rank_program(g, core, T, topo):
     g.sync.dma_start(T.G[:], T.gate[:]).then_inc(S.ldg, 16)
     g.scalar.dma_start(T.X[:, 0:B], T.x[:, 0:B]).then_inc(S.ldx0, 16)
     g.scalar.dma_start(T.X[:, B:2 * B], T.x[:, B:2 * B]).then_inc(S.ldx1, 16)
+    if rank != 0:
+        g.scalar.wait_ge(S.ldg, 16)
+        g.scalar.activation(T.pg1[:], T.G[:, B:2 * B], ActivationFunctionType.Copy).then_inc(S.a1, 1)
+        g.scalar.activation(T.pg0[:], T.G[:, 0:B], ActivationFunctionType.Copy).then_inc(S.a0, 1)
 
     calls1 = s1(rank)
     V.wait_ge(S.ldg, 16)
@@ -167,12 +198,16 @@ def rank_program(g, core, T, topo):
         if rest:
             chunks.append(rest)
         for k, c in enumerate(chunks):
+            ps = rank != 0 and (k > 0 or not calls1)
+            if ps:
+                V.wait_ge(S.a1, 1)
+            g1 = {j: (T.pg1[:, sl(j)] if ps else T.G[:, sl(j, B)]) for j in c}
             if rank != 0:
                 for j in c:
-                    tt(T.AB[:, sl(2 * j)], T.G[:, sl(j, B)], T.G[:, sl(j)], mult)
+                    tt(T.AB[:, sl(2 * j)], g1[j], T.G[:, sl(j)], mult)
             if k == 0:
                 V.wait_ge(S.ldx0, 16)
-            ti = [tt(T.pt[:, sl(j)], T.G[:, sl(j, B)], T.X[:, sl(j)], mult) for j in c]
+            ti = [tt(T.pt[:, sl(j)], g1[j], T.X[:, sl(j)], mult) for j in c]
             if k == 0:
                 V.wait_ge(S.ldx1, 16)
             for j, i in zip(c, ti):
@@ -183,6 +218,11 @@ def rank_program(g, core, T, topo):
             lo_col = W if rank == 0 else 0
             fused([(r, mask, size, T.AB[:, 2 * W * j + lo_col:2 * W * (j + 1)],
                     T.land1[:, 2 * W * me + lo_col:2 * W * (me + 1)], S["s1_%d" % me]) for j, r, mask, size in c])
+        for r, q in feed.items():
+            if q == rank:
+                gneed(max(bidx.values()))
+                stay = engines(rank)[2]
+                fused([(r, sum(stay), len(stay), T.AB[:], T.nland[:], S.nb)])
     else:
         V.wait_ge(S.ldx0, 16)
         V.wait_ge(S.ldx1, 16)
@@ -195,9 +235,13 @@ def rank_program(g, core, T, topo):
         g.sync.dma_start(T.y[:, 0:B], T.X[:, 0:B]).then_inc(S.st0, 16)
         g.scalar.wait_ge(S.v, i_y)
         g.scalar.dma_start(T.y[:, B:2 * B], T.ybuf[:, B:2 * B]).then_inc(S.st1, 16)
-    else:
-        vdo(V.tensor_copy(T.pg1[:], T.G[:, B:2 * B]))
-        i_g0 = vdo(V.tensor_copy(T.pg0[:], T.G[:, 0:B]))
+        nst[0] = 1
+
+    def whole(p):
+        return p[0][:, p[1]:p[1] + W]
+
+    def part(p, u):
+        return p[0][:, p[1] + u * (W // 2):p[1] + (u + 1) * (W // 2)]
 
     mA, mB, midx = {}, {}, {}
     if rank in owners[gi]:
@@ -212,58 +256,88 @@ def rank_program(g, core, T, topo):
         def comp(m):
             if grp[m] == rank:
                 need(bidx[j])
-                return T.AB[:, sl(2 * j)], T.AB[:, sl(2 * j + 1)]
+                return (T.AB, 2 * j * W), (T.AB, (2 * j + 1) * W)
             V.wait_ge(S["s1_%d" % m], arrived[m])
-            return T.land1[:, sl(2 * m)], T.land1[:, sl(2 * m + 1)]
+            return (T.land1, 2 * m * W), (T.land1, (2 * m + 1) * W)
 
         calls2 = s2(rank)
         if gi == 0:
             hloc, hidx = {}, {}
             last = len(grp)
             hloc[1] = comp(0)[1]
-            hidx[1] = 0
+            hidx[1] = [0, 0]
             for m in range(1, last):
                 a, b = comp(m)
-                p = T.pc[:, sl(m % 2)]
-                need(hidx[m])
-                need(tt(p, a, hloc[m], mult))
-                hloc[m + 1] = T.hland[:, sl(j)] if m + 1 == me else T.Hbuf[:, sl(m + 1)]
-                hidx[m + 1] = tt(hloc[m + 1], p, b, add)
+                p = (T.pc, (m % 2) * W)
+                ip = []
+                for u in (0, 1):
+                    need(hidx[m][u])
+                    ip.append(tt(part(p, u), part(a, u), part(hloc[m], u), mult))
+                hloc[m + 1] = (T.hland, j * W) if m + 1 == me else (T.Hbuf, (m + 1) * W)
+                hidx[m + 1] = []
+                for u in (0, 1):
+                    need(ip[u])
+                    hidx[m + 1].append(tt(part(hloc[m + 1], u), part(p, u), part(b, u), add))
             if me == 1:
-                i_own = vdo(V.tensor_copy(T.hland[:, sl(j)], hloc[1]))
+                i_own = vdo(V.tensor_copy(T.hland[:, sl(j)], whole(hloc[1])))
             elif me > 1:
-                i_own = hidx[me]
+                i_own = hidx[me][1]
             if me != 0:
                 g.wait_ge(S.s1_0, arrived[0])
             for c in calls2:
-                gneed(max(hidx[t[0]] for t in c))
-                fused([(r, mask, size, hloc[i], T.hland[:, sl(j)], S["s2_%d" % j]) for i, r, mask, size in c])
-            gneed(hidx[last])
-            farb, _nearb = engines(rank)
+                gneed(max(hidx[t[0]][1] for t in c))
+                fused([(r, mask, size, whole(hloc[i]), T.hland[:, sl(j)], S["s2_%d" % j])
+                       for i, r, mask, size in c])
+            farb = engines(rank)[0]
+            csem = S["c%d" % _half(j)]
+            i4 = grp.index(rest0[0])
+            gneed(hidx[i4][1])
+            fused([(rest0[_half(j)], sum(farb), len(farb), whole(hloc[i4]), T.cland[:, sl(j)], csem)])
+            gneed(hidx[last][1])
+            dst = cdst(j)
             g.remote_dma_fused([RemoteDMATransfer(
-                dst_ids=[did(r) for r in groups[1]], dma_engine_mask=sum(farb), remote_sem=S.car,
-                srcs=[hloc[last]], dsts=[T.cland[:, sl(j)] for r in groups[1]], alu_op=0)], local_sem=S.ls)
+                dst_ids=[did(r) for r in dst], dma_engine_mask=sum(farb), remote_sem=csem,
+                srcs=[whole(hloc[last])], dsts=[T.cland[:, sl(j)] for r in dst], alu_op=0)], local_sem=S.ls)
             ls[0] += len(farb)
         else:
-            mA[1], mB[1] = comp(0)
-            mfull = {1: T.AB[:, 2 * W * j:2 * W * (j + 1)] if me == 0 else T.land1[:, 0:2 * W]}
+            a, b = comp(0)
+            mA[1], mB[1] = whole(a), whole(b)
+            mfull = {}
             midx[1] = bidx[j] if me == 0 else 0
-            for m in range(1, len(grp) - 1):
+            for m in range(1, K):
                 a, b = comp(m)
                 p = T.pc[:, sl(m % 2)]
                 need(midx[m])
-                ip = tt(p, a, mB[m], mult)
+                ip = tt(p, whole(a), mB[m], mult)
                 mA[m + 1], mB[m + 1] = T.MB[:, sl(2 * m + 2)], T.MB[:, sl(2 * m + 3)]
                 mfull[m + 1] = T.MB[:, 2 * W * (m + 1):2 * W * (m + 2)]
-                tt(mA[m + 1], a, mA[m], mult)
+                tt(mA[m + 1], whole(a), mA[m], mult)
                 need(ip)
-                midx[m + 1] = tt(mB[m + 1], p, b, add)
-            if me != 0:
-                g.wait_ge(S.s1_0, arrived[0])
+                midx[m + 1] = tt(mB[m + 1], p, whole(b), add)
             for c in calls2:
                 gneed(max(midx[t[0]] for t in c))
                 fused([(r, mask, size, mfull[i], T.mland[:, 2 * W * j:2 * W * (j + 1)], S["s2_%d" % j])
                        for i, r, mask, size in c])
+
+    def close(lo, hi, P, Q, C):
+        mid = (lo + hi) // 2
+        rs = [(lo, mid), (mid, hi)]
+        i0 = [tt(T.pt[:, a:b], P[:, a:b], C[:, a:b], mult) for a, b in rs]
+        i1, i2, i3 = [], [], []
+        for (a, b), i in zip(rs, i0):
+            need(i)
+            i1.append(tt(T.ybuf[:, a:b], T.pt[:, a:b], Q[:, a:b], add))
+        for (a, b), i in zip(rs, i1):
+            need(i)
+            i2.append(tt(T.pm[:, a:b], T.pg1[:, a:b], T.ybuf[:, a:b], mult))
+        for (a, b), i in zip(rs, i2):
+            need(i)
+            i3.append(tt(T.ybuf[:, B + a:B + b], T.pm[:, a:b], T.X[:, B + a:B + b], add))
+        g.sync.wait_ge(S.v, i1[-1])
+        g.sync.dma_start(T.y[:, lo:hi], T.ybuf[:, lo:hi]).then_inc(S.st0, 16)
+        g.scalar.wait_ge(S.v, i3[-1])
+        g.scalar.dma_start(T.y[:, B + lo:B + hi], T.ybuf[:, B + lo:B + hi]).then_inc(S.st1, 16)
+        nst[0] += 1
 
     if rank != 0:
         cnt = {}
@@ -272,45 +346,57 @@ def rank_program(g, core, T, topo):
                 for t in c:
                     if t[1] == rank:
                         cnt[jj] = t[3]
-        ncar = sum(len(engines(o)[0]) for o in owners[0])
-        need(i_g0)
-        if gi == 1 and me != 0:
-            for jj in range(K):
-                if jj in cnt:
-                    V.wait_ge(S["s2_%d" % jj], cnt[jj])
-                    asrc, bsrc = T.mland[:, sl(2 * jj)], T.mland[:, sl(2 * jj + 1)]
-                else:
-                    need(midx[me])
-                    asrc, bsrc = mA[me], mB[me]
-                iq = tt(T.pm[:, sl(jj)], T.pg0[:, sl(jj)], bsrc, mult)
-                tt(T.pa[:, sl(jj)], T.pg0[:, sl(jj)], asrc, mult)
-                need(iq)
-                ic = tt(T.Q0[:, sl(jj)], T.pm[:, sl(jj)], T.X[:, sl(jj)], add)
-            V.wait_ge(S.car, ncar)
-            need(ic)
-            need(tt(T.pt[:], T.pa[:], T.cland[:], mult))
-            i_y0 = tt(T.ybuf[:, 0:B], T.pt[:], T.Q0[:], add)
+        need(vc[0])
+        V.wait_ge(S.a1, 1)
+        V.wait_ge(S.a0, 1)
+        if rank in owners[0]:
+            for jj in cnt:
+                V.wait_ge(S["s2_%d" % jj], cnt[jj])
+            need(i_own)
+            close(0, B, T.pg0, T.X, T.hland)
         else:
-            if gi == 1:
-                V.wait_ge(S.car, ncar)
-                h = T.cland
+            P, Q = T.pg0, T.X
+            if rank in feed:
+                V.wait_ge(S.nb, len(engines(feed[rank])[2]))
+                iq = [tt(T.pm[:, sl(jj)], T.pg0[:, sl(jj)], T.nland[:, sl(2 * jj + 1)], mult) for jj in range(K)]
+                for jj in range(K):
+                    tt(T.pn[:, sl(jj)], T.pg0[:, sl(jj)], T.nland[:, sl(2 * jj)], mult)
+                need(iq[-1])
+                need(tt(T.Qn[:], T.pm[:], T.X[:, 0:B], add))
+                P, Q = T.pn, T.Qn
+            if gi == 1 and me >= 2:
+                for jj in range(K):
+                    if jj not in cnt:
+                        need(midx[me])
+                        asrc, bsrc = mA[me], mB[me]
+                    else:
+                        V.wait_ge(S["s2_%d" % jj], cnt[jj])
+                        asrc, bsrc = T.mland[:, sl(2 * jj)], T.mland[:, sl(2 * jj + 1)]
+                    iq = tt(T.pm[:, sl(jj)], P[:, sl(jj)], bsrc, mult)
+                    tt(T.pa[:, sl(jj)], P[:, sl(jj)], asrc, mult)
+                    need(iq)
+                    ic = tt(T.Q0[:, sl(jj)], T.pm[:, sl(jj)], Q[:, sl(jj)], add)
+                need(ic)
+                P, Q = T.pa, T.Q0
+            direct = [sum(len(engines(o)[0]) for jj, o in enumerate(owners[0]) if _half(jj) == hh) for hh in (0, 1)]
+            if rank in swap:
+                pos, nb = swap[rank]
+                lo, hi = pos * B // 2, (pos + 1) * B // 2
+                mine = [b for b in engines(rank)[0] if b & topo.mask(core, cores[nb])]
+                g.wait_ge(S["c%d" % pos], direct[pos])
+                fused([(nb, sum(mine), len(mine), T.cland[:, lo:hi], T.cland[:, lo:hi], S["c%d" % pos])])
+                V.wait_ge(S["c%d" % pos], direct[pos])
+                close(lo, hi, P, Q, T.cland)
+                theirs = [b for b in engines(nb)[0] if b & topo.mask(cores[nb], core)]
+                V.wait_ge(S["c%d" % (1 - pos)], len(theirs))
+                close(B // 2 - lo, B - lo, P, Q, T.cland)
             else:
-                for jj in cnt:
-                    V.wait_ge(S["s2_%d" % jj], cnt[jj])
-                need(i_own)
-                h = T.hland
-            need(tt(T.pm[:], T.pg0[:], h[:], mult))
-            i_y0 = tt(T.ybuf[:, 0:B], T.pm[:], T.X[:, 0:B], add)
-        need(i_y0)
-        need(tt(T.pt[:], T.pg1[:], T.ybuf[:, 0:B], mult))
-        i_y1 = tt(T.ybuf[:, B:2 * B], T.pt[:], T.X[:, B:2 * B], add)
-        g.sync.wait_ge(S.v, i_y0)
-        g.sync.dma_start(T.y[:, 0:B], T.ybuf[:, 0:B]).then_inc(S.st0, 16)
-        g.scalar.wait_ge(S.v, i_y1)
-        g.scalar.dma_start(T.y[:, B:2 * B], T.ybuf[:, B:2 * B]).then_inc(S.st1, 16)
+                for hh in (0, 1):
+                    V.wait_ge(S["c%d" % hh], direct[hh])
+                close(0, B, P, Q, T.cland)
 
-    g.sync.wait_ge(S.st0, 16)
-    g.scalar.wait_ge(S.st1, 16)
+    g.sync.wait_ge(S.st0, 16 * nst[0])
+    g.scalar.wait_ge(S.st1, 16 * nst[0])
     g.wait_ge(S.v, vc[0])
     if ls[0]:
         g.wait_ge(S.ls, ls[0])

from concourse.bass import DstId, RemoteDMATransfer
from concourse.mybir import AluOpType, ActivationFunctionType

B = 512
K = 4
W = B // K
NEAR = 4

SCRATCH = {
    "G": ("sbuf", [128, 2 * B], "bfloat16"),
    "X": ("sbuf", [128, 2 * B], "bfloat16"),
    "AB": ("sbuf", [128, 2 * B], "bfloat16"),
    "land1": ("sbuf", [128, 6 * 2 * W], "bfloat16"),
    "Hbuf": ("sbuf", [128, 7 * W], "bfloat16"),
    "MB": ("sbuf", [128, 6 * 2 * W], "bfloat16"),
    "mland": ("sbuf", [128, K * 2 * W], "bfloat16"),
    "nland": ("sbuf", [128, K * 2 * W], "bfloat16"),
    "cland": ("sbuf", [128, B], "bfloat16"),
    "hland": ("sbuf", [128, B], "bfloat16"),
    "ybuf": ("sbuf", [128, 2 * B], "bfloat16"),
    "Qn": ("sbuf", [128, B], "float32"),
    "Q0": ("sbuf", [128, B], "float32"),
    "pn": ("psum", [128, B], "float32"),
    "pa": ("psum", [128, B], "float32"),
    "pg1": ("psum", [128, B], "float32"),
    "pg0": ("psum", [128, B], "float32"),
    "pt": ("psum", [128, B], "float32"),
    "pm": ("psum", [128, B], "float32"),
    "pc": ("psum", [128, B], "float32"),
}
SEMAPHORES = (["ldg", "ldx0", "ldx1", "v", "a0", "a1", "nb", "c0", "c1", "ls", "st0", "st1"]
              + ["s1_%d" % m for m in range(6)] + ["s2_%d" % j for j in range(K)])


def _bits(mask):
    return [1 << i for i in range(mask.bit_length()) if (mask >> i) & 1]


def _share(bits, n):
    size = 1
    while size * 2 * n <= len(bits):
        size *= 2
    return [sum(bits[i * size:(i + 1) * size]) for i in range(n)], size


def _half(j):
    return j * 2 // K


def _plan(T, topo):
    cores = list(T.cores)
    n = len(cores)
    groups = [list(range(n // 2)), list(range(n // 2, n))]
    chip = [topo.chip(c) for c in cores]
    owners = [groups[0][:K], groups[1][:K]]
    rest0 = [r for r in groups[0] if r not in owners[0]]
    rest1 = [r for r in groups[1] if r not in owners[1]]
    feed = {rest0[1]: rest0[0], groups[1][1]: groups[1][0], rest1[1]: rest1[0]}

    def engines(q):
        far, near = None, 0
        for r in range(n):
            if r == q:
                continue
            m = topo.mask(cores[q], cores[r])
            if chip[r] != chip[q]:
                far = m if far is None else far & m
            else:
                near |= m
        stay = [b for b in _bits(near) if not (b & far)]
        return _bits(far), stay[:NEAR], stay

    duo2, solo2 = [], []
    for r in groups[1]:
        same = [q for q in groups[1] if chip[q] == chip[r]]
        if same[0] != r:
            continue
        if len(same) == 2 and (n - 1) not in same:
            duo2.append(same)
        else:
            solo2.extend(same)
    swap = {}
    for duo in [rest0] + duo2:
        swap[duo[0]] = (0, duo[1])
        swap[duo[1]] = (1, duo[0])

    def cdst(j):
        return [duo[_half(j)] for duo in duo2] + solo2

    def pairs(q, dst, per_call):
        off = [d for d in dst if chip[d[1]] != chip[q]]
        on = [d for d in dst if chip[d[1]] == chip[q]]
        farb, nearb, _all = engines(q)
        calls = []
        for i in range(0, len(off), per_call):
            part = off[i:i + per_call]
            masks, size = _share(farb, len(part))
            calls.append([(key, r, masks[k], size) for k, (key, r) in enumerate(part)])
        if on:
            masks, size = _share(nearb, len(on))
            extra = [(key, r, masks[k], size) for k, (key, r) in enumerate(on)]
            if calls:
                calls[0].extend(extra)
            else:
                calls.append(extra)
        return calls

    def s1(q):
        if q in rest1:
            return []
        own = owners[0 if q in groups[0] else 1]
        dst = [(j, own[j]) for j in range(K) if own[j] != q]
        off = [d for d in dst if chip[d[1]] != chip[q]]
        on = [d for d in dst if chip[d[1]] == chip[q]]
        farb, nearb, _all = engines(q)
        ncalls = (len(off) + 1) // 2
        per = len(farb) // max(1, ncalls)
        calls = []
        for i in range(ncalls):
            part = off[2 * i:2 * i + 2]
            masks, size = _share(farb[i * per:(i + 1) * per], len(part))
            calls.append([(key, r, masks[k], size) for k, (key, r) in enumerate(part)])
        if on:
            masks, size = _share(nearb, len(on))
            calls.append([(key, r, masks[k], size) for k, (key, r) in enumerate(on)])
        return calls

    def s2(o):
        gi = 0 if o in groups[0] else 1
        if gi == 1:
            dst = [(min(i, K), r) for i, r in enumerate(groups[1]) if r != o and i >= 2]
            return pairs(o, dst, 2)
        early = [(i, r) for i, r in enumerate(groups[0]) if r != o and i != 0 and r in owners[0]]
        return pairs(o, early, max(1, len(early)))

    return cores, groups, owners, rest0, feed, swap, cdst, engines, s1, s2


def rank_program(g, core, T, topo):
    rank = T.rank_of(core)
    if rank is None:
        return
    cores, groups, owners, rest0, feed, swap, cdst, engines, s1, s2 = _plan(T, topo)
    n = len(cores)
    gi = 0 if rank in groups[0] else 1
    grp = groups[gi]
    me = grp.index(rank)
    S, V = T.sem, g.vector
    mult, add = AluOpType.mult, AluOpType.add
    vc, vseen, gseen, ls, nst = [0], [0], [0], [0], [0]

    def vdo(ins):
        ins.then_inc(S.v, 1)
        vc[0] += 1
        return vc[0]

    def need(i):
        if i > vseen[0]:
            V.wait_ge(S.v, i)
            vseen[0] = i

    def gneed(i):
        if i > gseen[0]:
            g.wait_ge(S.v, i)
            gseen[0] = i

    def tt(out, a, b, op):
        return vdo(V.tensor_tensor(out, a, b, op))

    def sl(j, base=0):
        return slice(base + j * W, base + (j + 1) * W)

    def did(r):
        rid, pid, _se = topo.addr(cores[r])
        return DstId(rid=rid, pnc=pid)

    def fused(items):
        trs = []
        for r, mask, size, src, dst, sem in items:
            trs.append(RemoteDMATransfer(dst_ids=[did(r)], dma_engine_mask=mask, remote_sem=sem, src=src, dst=dst))
            ls[0] += size
        g.remote_dma_fused(trs, local_sem=S.ls)

    g.sync.dma_start(T.G[:], T.gate[:]).then_inc(S.ldg, 16)
    g.scalar.dma_start(T.X[:, 0:B], T.x[:, 0:B]).then_inc(S.ldx0, 16)
    g.scalar.dma_start(T.X[:, B:2 * B], T.x[:, B:2 * B]).then_inc(S.ldx1, 16)
    if rank != 0:
        g.scalar.wait_ge(S.ldg, 16)
        g.scalar.activation(T.pg1[:], T.G[:, B:2 * B], ActivationFunctionType.Copy).then_inc(S.a1, 1)
        g.scalar.activation(T.pg0[:], T.G[:, 0:B], ActivationFunctionType.Copy).then_inc(S.a0, 1)

    calls1 = s1(rank)
    V.wait_ge(S.ldg, 16)
    bidx = {}
    if rank != n - 1:
        chunks = [[t[0] for t in c] for c in calls1]
        rest = [j for j in range(K) if all(j not in c for c in chunks)]
        if rest:
            chunks.append(rest)
        for k, c in enumerate(chunks):
            ps = rank != 0 and (k > 0 or not calls1)
            if ps:
                V.wait_ge(S.a1, 1)
            g1 = {j: (T.pg1[:, sl(j)] if ps else T.G[:, sl(j, B)]) for j in c}
            if rank != 0:
                for j in c:
                    tt(T.AB[:, sl(2 * j)], g1[j], T.G[:, sl(j)], mult)
            if k == 0:
                V.wait_ge(S.ldx0, 16)
            ti = [tt(T.pt[:, sl(j)], g1[j], T.X[:, sl(j)], mult) for j in c]
            if k == 0:
                V.wait_ge(S.ldx1, 16)
            for j, i in zip(c, ti):
                need(i)
                bidx[j] = tt(T.AB[:, sl(2 * j + 1)], T.pt[:, sl(j)], T.X[:, sl(j, B)], add)
        for c in calls1:
            gneed(max(bidx[t[0]] for t in c))
            lo_col = W if rank == 0 else 0
            fused([(r, mask, size, T.AB[:, 2 * W * j + lo_col:2 * W * (j + 1)],
                    T.land1[:, 2 * W * me + lo_col:2 * W * (me + 1)], S["s1_%d" % me]) for j, r, mask, size in c])
        for r, q in feed.items():
            if q == rank:
                gneed(max(bidx.values()))
                stay = engines(rank)[2]
                fused([(r, sum(stay), len(stay), T.AB[:], T.nland[:], S.nb)])
    else:
        V.wait_ge(S.ldx0, 16)
        V.wait_ge(S.ldx1, 16)

    i_own = 0
    if rank == 0:
        need(max(bidx.values()))
        i_y = tt(T.ybuf[:, B:2 * B], T.pt[:], T.X[:, B:2 * B], add)
        g.sync.wait_ge(S.ldx0, 16)
        g.sync.dma_start(T.y[:, 0:B], T.X[:, 0:B]).then_inc(S.st0, 16)
        g.scalar.wait_ge(S.v, i_y)
        g.scalar.dma_start(T.y[:, B:2 * B], T.ybuf[:, B:2 * B]).then_inc(S.st1, 16)
        nst[0] = 1

    def whole(p):
        return p[0][:, p[1]:p[1] + W]

    def part(p, u):
        return p[0][:, p[1] + u * (W // 2):p[1] + (u + 1) * (W // 2)]

    mA, mB, midx = {}, {}, {}
    if rank in owners[gi]:
        j = owners[gi].index(rank)
        arrived = {}
        for m, q in enumerate(grp):
            for c in s1(q):
                for t in c:
                    if t[1] == rank:
                        arrived[m] = t[3]

        def comp(m):
            if grp[m] == rank:
                need(bidx[j])
                return (T.AB, 2 * j * W), (T.AB, (2 * j + 1) * W)
            V.wait_ge(S["s1_%d" % m], arrived[m])
            return (T.land1, 2 * m * W), (T.land1, (2 * m + 1) * W)

        calls2 = s2(rank)
        if gi == 0:
            hloc, hidx = {}, {}
            last = len(grp)
            hloc[1] = comp(0)[1]
            hidx[1] = [0, 0]
            for m in range(1, last):
                a, b = comp(m)
                p = (T.pc, (m % 2) * W)
                ip = []
                for u in (0, 1):
                    need(hidx[m][u])
                    ip.append(tt(part(p, u), part(a, u), part(hloc[m], u), mult))
                hloc[m + 1] = (T.hland, j * W) if m + 1 == me else (T.Hbuf, (m + 1) * W)
                hidx[m + 1] = []
                for u in (0, 1):
                    need(ip[u])
                    hidx[m + 1].append(tt(part(hloc[m + 1], u), part(p, u), part(b, u), add))
            if me == 1:
                i_own = vdo(V.tensor_copy(T.hland[:, sl(j)], whole(hloc[1])))
            elif me > 1:
                i_own = hidx[me][1]
            if me != 0:
                g.wait_ge(S.s1_0, arrived[0])
            for c in calls2:
                gneed(max(hidx[t[0]][1] for t in c))
                fused([(r, mask, size, whole(hloc[i]), T.hland[:, sl(j)], S["s2_%d" % j])
                       for i, r, mask, size in c])
            farb = engines(rank)[0]
            csem = S["c%d" % _half(j)]
            i4 = grp.index(rest0[0])
            gneed(hidx[i4][1])
            fused([(rest0[_half(j)], sum(farb), len(farb), whole(hloc[i4]), T.cland[:, sl(j)], csem)])
            gneed(hidx[last][1])
            dst = cdst(j)
            g.remote_dma_fused([RemoteDMATransfer(
                dst_ids=[did(r) for r in dst], dma_engine_mask=sum(farb), remote_sem=csem,
                srcs=[whole(hloc[last])], dsts=[T.cland[:, sl(j)] for r in dst], alu_op=0)], local_sem=S.ls)
            ls[0] += len(farb)
        else:
            a, b = comp(0)
            mA[1], mB[1] = whole(a), whole(b)
            mfull = {}
            midx[1] = bidx[j] if me == 0 else 0
            for m in range(1, K):
                a, b = comp(m)
                p = T.pc[:, sl(m % 2)]
                need(midx[m])
                ip = tt(p, whole(a), mB[m], mult)
                mA[m + 1], mB[m + 1] = T.MB[:, sl(2 * m + 2)], T.MB[:, sl(2 * m + 3)]
                mfull[m + 1] = T.MB[:, 2 * W * (m + 1):2 * W * (m + 2)]
                tt(mA[m + 1], whole(a), mA[m], mult)
                need(ip)
                midx[m + 1] = tt(mB[m + 1], p, whole(b), add)
            for c in calls2:
                gneed(max(midx[t[0]] for t in c))
                fused([(r, mask, size, mfull[i], T.mland[:, 2 * W * j:2 * W * (j + 1)], S["s2_%d" % j])
                       for i, r, mask, size in c])

    def close(lo, hi, P, Q, C):
        mid = (lo + hi) // 2
        rs = [(lo, mid), (mid, hi)]
        i0 = [tt(T.pt[:, a:b], P[:, a:b], C[:, a:b], mult) for a, b in rs]
        i1, i2, i3 = [], [], []
        for (a, b), i in zip(rs, i0):
            need(i)
            i1.append(tt(T.ybuf[:, a:b], T.pt[:, a:b], Q[:, a:b], add))
        for (a, b), i in zip(rs, i1):
            need(i)
            i2.append(tt(T.pm[:, a:b], T.pg1[:, a:b], T.ybuf[:, a:b], mult))
        for (a, b), i in zip(rs, i2):
            need(i)
            i3.append(tt(T.ybuf[:, B + a:B + b], T.pm[:, a:b], T.X[:, B + a:B + b], add))
        g.sync.wait_ge(S.v, i1[-1])
        g.sync.dma_start(T.y[:, lo:hi], T.ybuf[:, lo:hi]).then_inc(S.st0, 16)
        g.scalar.wait_ge(S.v, i3[-1])
        g.scalar.dma_start(T.y[:, B + lo:B + hi], T.ybuf[:, B + lo:B + hi]).then_inc(S.st1, 16)
        nst[0] += 1

    if rank != 0:
        cnt = {}
        for jj, o in enumerate(owners[gi]):
            for c in (s2(o) if o != rank else []):
                for t in c:
                    if t[1] == rank:
                        cnt[jj] = t[3]
        need(vc[0])
        V.wait_ge(S.a1, 1)
        V.wait_ge(S.a0, 1)
        if rank in owners[0]:
            for jj in cnt:
                V.wait_ge(S["s2_%d" % jj], cnt[jj])
            need(i_own)
            close(0, B, T.pg0, T.X, T.hland)
        else:
            P, Q = T.pg0, T.X
            if rank in feed:
                V.wait_ge(S.nb, len(engines(feed[rank])[2]))
                iq = [tt(T.pm[:, sl(jj)], T.pg0[:, sl(jj)], T.nland[:, sl(2 * jj + 1)], mult) for jj in range(K)]
                for jj in range(K):
                    tt(T.pn[:, sl(jj)], T.pg0[:, sl(jj)], T.nland[:, sl(2 * jj)], mult)
                need(iq[-1])
                need(tt(T.Qn[:], T.pm[:], T.X[:, 0:B], add))
                P, Q = T.pn, T.Qn
            if gi == 1 and me >= 2:
                for jj in range(K):
                    if jj not in cnt:
                        need(midx[me])
                        asrc, bsrc = mA[me], mB[me]
                    else:
                        V.wait_ge(S["s2_%d" % jj], cnt[jj])
                        asrc, bsrc = T.mland[:, sl(2 * jj)], T.mland[:, sl(2 * jj + 1)]
                    iq = tt(T.pm[:, sl(jj)], P[:, sl(jj)], bsrc, mult)
                    tt(T.pa[:, sl(jj)], P[:, sl(jj)], asrc, mult)
                    need(iq)
                    ic = tt(T.Q0[:, sl(jj)], T.pm[:, sl(jj)], Q[:, sl(jj)], add)
                need(ic)
                P, Q = T.pa, T.Q0
            direct = [sum(len(engines(o)[0]) for jj, o in enumerate(owners[0]) if _half(jj) == hh) for hh in (0, 1)]
            if rank in swap:
                pos, nb = swap[rank]
                lo, hi = pos * B // 2, (pos + 1) * B // 2
                mine = [b for b in engines(rank)[0] if b & topo.mask(core, cores[nb])]
                g.wait_ge(S["c%d" % pos], direct[pos])
                fused([(nb, sum(mine), len(mine), T.cland[:, lo:hi], T.cland[:, lo:hi], S["c%d" % pos])])
                V.wait_ge(S["c%d" % pos], direct[pos])
                close(lo, hi, P, Q, T.cland)
                theirs = [b for b in engines(nb)[0] if b & topo.mask(cores[nb], core)]
                V.wait_ge(S["c%d" % (1 - pos)], len(theirs))
                close(B // 2 - lo, B - lo, P, Q, T.cland)
            else:
                for hh in (0, 1):
                    V.wait_ge(S["c%d" % hh], direct[hh])
                close(0, B, P, Q, T.cland)

    g.sync.wait_ge(S.st0, 16 * nst[0])
    g.scalar.wait_ge(S.st1, 16 * nst[0])
    g.wait_ge(S.v, vc[0])
    if ls[0]:
        g.wait_ge(S.ls, ls[0])
